import numpy as np
import ml_dtypes


def mxq(x, axis, fmt="e4m3"):
    dtype, down = {"e4m3": (ml_dtypes.float8_e4m3fn, 7), "e5m2": (ml_dtypes.float8_e5m2, 14)}[fmt]
    v = np.moveaxis(np.asarray(x, np.float32).astype(ml_dtypes.bfloat16).astype(np.float64), axis, -1)
    blocks = v.reshape(v.shape[:-1] + (-1, 32))
    amax = np.abs(blocks).max(-1, keepdims=True)
    byte = np.maximum(np.where(amax > 0, np.frexp(amax)[1] - 1 + 127, 0) - down, 1)
    scale = np.exp2(byte - 127.0)
    codes = (blocks / scale).astype(np.float32).astype(dtype).astype(np.float64)
    return np.moveaxis((codes * scale).reshape(v.shape), -1, axis)


WIDE = False


def mx_kscale(k):
    if not WIDE:
        return np.ones(k)
    levels = np.array([10, -10, 5, -5, 0])
    if k % 512:
        return np.exp2(np.random.permutation(np.resize(levels, k // 32))).repeat(32)
    a = np.empty((k // 512, 16))
    for p in range(k // 512):
        a[p, :8] = np.random.permutation(np.resize(levels, 8))
        for g in range(8):
            far = levels[np.abs(levels - a[p, g]) >= 10]
            a[p, g + 8] = far[np.random.randint(len(far))]
    return np.exp2(a.ravel()).repeat(32)


BF16 = ml_dtypes.bfloat16


def bf(x):
    return np.asarray(x, np.float32).astype(BF16)


def f64(x):
    return np.asarray(x).astype(np.float64)


E2M1 = np.array([0.0, 0.5, 1.0, 1.5, 2.0, 3.0, 4.0, 6.0, -0.0, -0.5, -1.0, -1.5, -2.0, -3.0, -4.0, -6.0])


def pack_weight(w, fmt):
    k, n = w.shape
    w = f64(bf(w)).reshape(k // 32, 32, n)
    amax = np.abs(w).max(1)
    if fmt == "e4m3":
        byte = np.frexp(amax)[1] - 1 + 127 - 7
    else:
        mant, ex = np.frexp(amax / 6.0)
        byte = np.where(mant > 0.5, ex, ex - 1) + 127
    byte = np.clip(np.where(amax > 0, byte, 1), 1, 254)
    scaled = (w * np.exp2(127.0 - byte)[:, None, :]).reshape(k, n).astype(np.float32)
    by_word = np.ascontiguousarray(scaled.reshape(k // 512, 128, 4, n).transpose(0, 1, 3, 2))
    if fmt == "e4m3":
        words = by_word.astype(ml_dtypes.float8_e4m3fn).view(np.uint8)
    else:
        c = by_word.astype(ml_dtypes.float4_e2m1fn).view(np.uint8) & 0xF
        words = c[..., 0::2] | (c[..., 1::2] << 4)
    return np.ascontiguousarray(words), np.ascontiguousarray(byte.astype(np.uint8).reshape(k // 512, 16, n))


def unpack_weight(words, scales, fmt):
    g, p, n, _ = words.shape
    if fmt == "e4m3":
        vals = np.ascontiguousarray(words).view(ml_dtypes.float8_e4m3fn).astype(np.float64)
    else:
        nib = np.empty((g, p, n, 4), np.uint8)
        nib[..., 0::2] = words & 0xF
        nib[..., 1::2] = words >> 4
        vals = E2M1[nib]
    vals = vals * np.repeat(np.exp2(scales.astype(np.float64) - 127.0), 8, axis=1)[..., None]
    return vals.transpose(0, 1, 3, 2).reshape(g * 512, n)
def pack4(w):
    words, scales = pack_weight(w, "e2m1")
    return words.reshape(words.shape[0], 128, -1), scales


def unpack4(words, scales):
    return unpack_weight(words.reshape(words.shape[0], 128, -1, 2), scales, "e2m1")


def planes(Y):
    n, m = Y.shape
    b = f64(bf(Y)).reshape(n // 32, 32, m)
    amax = np.abs(b).max(1)
    byte = np.clip(np.where(amax > 0, np.frexp(amax)[1] - 1 + 127 - 7, 1), 1, 254)
    codes = (b * np.exp2(127.0 - byte)[:, None, :]).reshape(n, m).astype(np.float32).astype(ml_dtypes.float8_e4m3fn).view(np.uint8)
    words = codes.reshape(n // 512, 128, 4, m).transpose(0, 1, 3, 2)
    return np.ascontiguousarray(words), np.ascontiguousarray(byte.astype(np.uint8).reshape(n // 512, 16, m))


N, D, O, P = 1024, 1024, 1024, 1024


def setup_inputs():
    s, t = mx_kscale(D), mx_kscale(N)
    x = np.random.standard_normal((N, D)) * s
    h = np.random.standard_normal((D, O)) / np.sqrt(D) / s[:, None]
    b = 0.5 * np.random.standard_normal(O)
    a = np.random.standard_normal((N, P)) / np.sqrt(N) / t[:, None]
    w = (1.0 + 0.1 * np.random.standard_normal(N)) * t
    rho = np.random.uniform(0.2, 1.0, (P, O))
    h_words, h_scales = pack4(h)
    return {"x": bf(x), "h_words": h_words, "h_scales": h_scales, "b": bf(b), "a": bf(a), "w": bf(w), "rho": bf(rho)}


def observe(x, h_words, h_scales, b):
    return np.tanh((mxq(f64(x), 1, "e4m3") @ unpack4(h_words, h_scales)) + f64(b)[None, :])


def core(x, h_words, h_scales, b, a, w, rho):
    y = observe(x, h_words, h_scales, b)
    c = y - np.mean(y, axis=0, keepdims=True)
    e = c * f64(w)[:, None]
    p = mxq(f64(a), 0, "e4m3").T @ mxq(e, 0, "e4m3")
    cov = f64(rho) * p
    return cov


def reference(x, h_words, h_scales, b, a, w, rho):
    R_out = core(x, h_words, h_scales, b, a, w, rho)
    words, scales = planes(R_out)
    return R_out, words, scales

@@ -1,0 +1,307 @@
+from contextlib import ExitStack
+
+import concourse.mybir as mybir
+from concourse.masks import make_identity
+
+F32 = mybir.dt.float32
+BF16 = mybir.dt.bfloat16
+I32 = mybir.dt.int32
+U32 = mybir.dt.uint32
+U8 = mybir.dt.uint8
+E4M3 = mybir.dt.float8_e4m3fn_x4
+E2M1 = mybir.dt.float4_e2m1fn_x4
+TANH = mybir.ActivationFunctionType.Tanh
+ADD = mybir.AluOpType.add
+SUB = mybir.AluOpType.subtract
+MUL = mybir.AluOpType.mult
+
+P = 128
+N = 1024
+FLOPS = 2 * 2 * N * N * N
+
+
+ORDER = """
+XT001.P XT000.P XC001.V WM.P XC000.S XQ001.V XT010.P XQ000.V WC.S XT011.P XC010.V XC011.V XQ010.V XQ011.V
+M100.P AI001.V AI011.S M140.P AI010.V M110.P TH00.S AI000.V XT100.P TH40.S AQ01.V XT101.P XC100.S AQ00.V
+M130.P XC101.S XQ100.V XT110.P TH30.S XQ101.V XT111.P XC110.V TH10.S M120.P XC111.V AI110.S M160.P AI101.V
+M170.P XQ110.V TH60.S XQ111.V AI111.V TH70.S M121.P AI100.V TH20.S M101.P AQ11.V TH21.S M111.P AQ10.V TH01.S
+M171.P ME2.G ST2.V TH11.S M141.P ME0.G TH71.S M131.P ME1.G ST0.V TH41.S ET2.P ME7.G M151.P TH31.S ST1.V ME4.G
+ET0.P EC2.S ME3.G M161.P ST3.V EC0.S ET1.P TH61.S M150.P ST7.V EC1.S ME6.G ET3.P TH50.S EQ01.V ET7.P EQ00.V
+EC3.S ST4.V M2001.P EC7.S M2011.P TH51.S EQ11.V M2000.P EQ10.V PC011.S ME5.G TT001.V ET4.P ST5.V M2111.P EC4.S
+M2100.P PC111.S TT000.V TT011.G ET5.P TT100.V GR001.S M2101.P EC5.V TT111.G GR000.S M2010.P TT101.V M2110.P
+TT010.V GR101.S SF10.D EQ20.V GR100.S OQ00.V EQ21.V GR011.S OQ10.V M2211.P TT110.V GR010.S M2201.P ST6.V
+SF11.D PC211.S M2210.P GR110.S M2200.P TT210.V TT211.G GR111.S ET6.P TT201.V EC6.S OQ11.V SF21.D GR210.V SC1.D
+EQ30.V EQ31.V OQ01.V M2301.P TT200.V GR211.G SC0.D SS0.D M2311.P TT301.V GR200.S SF20.D M2310.P GR201.V
+TT311.V M2300.P TT310.V TT300.V GR310.G SF31.D GR301.S SF30.D GR311.V GR300.G OQ31.V OQ30.V OQ20.V SC3.D
+OQ21.V SC2.D SS1.D
+"""
+
+
+def mark(token):
+    return token
+
+
+def tile_localisedweightedcrossmoment_kernel(tc, x, h_words, h_scales, b, a, w, rho, out_0, out_1, out_2):
+    nc = tc.nc
+    with ExitStack() as ctx:
+        ctx.enter_context(tc.manual_schedule())
+        keep = ctx.enter_context(tc.tile_pool(name="keep", bufs=1))
+        et_pool = ctx.enter_context(tc.tile_pool(name="et_pool", bufs=3))
+        og_pool = ctx.enter_context(tc.tile_pool(name="og_pool", bufs=4))
+        ps_tr = ctx.enter_context(tc.psum_pool(name="ps_tr", bufs=2))
+        ps_one = ctx.enter_context(tc.psum_pool(name="ps_one", bufs=3))
+        ps_two = ctx.enter_context(tc.psum_pool(name="ps_two", bufs=3))
+
+        ident = keep.tile([P, P], F32, align_bytes=64, name="ident")
+        make_identity(nc, ident[:])
+        hs = keep.tile([P, 2, N], U8, align_bytes=64, name="hs")
+        wz = keep.tile([P, N], BF16, align_bytes=64, name="wz")
+        bz = keep.tile([P, P], BF16, align_bytes=64, name="bz")
+        ones = keep.tile([P, P], BF16, align_bytes=64, name="ones")
+        nc.vector.memset(hs[:].bitcast(I32), 0)
+        nc.vector.memset(wz[:].bitcast(I32), 0)
+        nc.vector.memset(bz[:].bitcast(I32), 0)
+        nc.gpsimd.memset(ones[:], 1.0)
+        ident_bf = keep.tile([P, P], BF16, align_bytes=64, name="ident_bf")
+
+        x_raw = [[keep.tile([P, 2, N], BF16, align_bytes=64, name="x_raw%d%d" % (g, u)) for u in range(2)] for g in range(2)]
+        a_raw = [keep.tile([P, 4, N], BF16, align_bytes=64, name="a_raw%d" % g) for g in range(2)]
+        rho_sb = [keep.tile([P, 4, N], BF16, align_bytes=64, name="rho_sb%d" % g) for g in range(2)]
+        h_sb = keep.tile([P, 2, 2 * N], U8, align_bytes=64, name="h_sb")
+
+        def load_x(g, u):
+            src = x[512 * g : 512 * (g + 1), :].rearrange("(p j) d -> p j d", j=4)
+            nc.sync.dma_start(out=x_raw[g][u][:], in_=src[:, 2 * u : 2 * u + 2, :])
+
+        def load_rows(dst, src, g):
+            nc.sync.dma_start(out=dst[g][:], in_=src[512 * g : 512 * (g + 1), :].rearrange("(p j) d -> p j d", j=4))
+
+        def load_h():
+            nc.sync.dma_start(out=h_sb[:].bitcast(I32), in_=h_words.bitcast(I32).rearrange("g p c -> p g c"))
+
+        def load_hs(queue):
+            for q in range(4):
+                queue.dma_start(
+                    out=hs[32 * q : 32 * q + 4, :, :].bitcast(I32),
+                    in_=h_scales.bitcast(I32)[:, 4 * q : 4 * q + 4, :].rearrange("g q n -> q g n"),
+                )
+
+        def load_wb(queue):
+            queue.dma_start(out=wz[0:1, :], in_=w.rearrange("(r n) -> r n", r=1))
+            queue.dma_start(out=bz[0:8, :], in_=b.rearrange("(c p) -> c p", p=P))
+
+        load_wb(nc.gpsimd)
+        load_x(0, 0)
+        load_x(0, 1)
+        load_hs(nc.sync)
+        load_h()
+        load_rows(a_raw, a, 0)
+        load_x(1, 0)
+        load_x(1, 1)
+        load_rows(a_raw, a, 1)
+        load_rows(rho_sb, rho, 0)
+        load_rows(rho_sb, rho, 1)
+        warm = keep.tile([P, 1], F32, name="warm")
+        nc.scalar.activation(out=warm[:], in_=ident[:, 0:1], func=TANH)
+        nc.vector.tensor_copy(out=ident_bf[:], in_=ident[:])
+
+        xg = keep.tile([P, 2, 4 * N], BF16, align_bytes=64, name="xg")
+        xc = keep.tile([P, 2, N], U32, align_bytes=64, name="xc")
+        xs = keep.tile([P, 2, N], U8, align_bytes=64, name="xs")
+        ag = [keep.tile([P, N, 4], BF16, align_bytes=64, name="ag%d" % g) for g in range(2)]
+        ac = [keep.tile([P, N], U32, align_bytes=64, name="ac%d" % g) for g in range(2)]
+        asc = [keep.tile([P, N], U8, align_bytes=64, name="asc%d" % g) for g in range(2)]
+        b_col = keep.tile([P, 8], F32, name="b_col")
+        w_bc = keep.tile([P, N], BF16, align_bytes=64, name="w_bc")
+        y = [keep.tile([P, N], F32, align_bytes=64, name="y%d" % i) for i in range(8)]
+        sums = keep.tile([P, 16], F32, name="sums")
+        mean = keep.tile([P, 8], F32, name="mean")
+        eg = [keep.tile([P, 2, 256, 4], BF16, align_bytes=64, name="eg%d" % i) for i in range(4)]
+        ec = [keep.tile([P, 2, 256], U32, align_bytes=64, name="ec%d" % i) for i in range(4)]
+        es = [keep.tile([P, 2, 256], U8, align_bytes=64, name="es%d" % i) for i in range(4)]
+        osc = [keep.tile([P, 2, 512], U8, align_bytes=64, name="osc%d" % i) for i in range(2)]
+        of = [[keep.tile([P, 4, 512], F32, align_bytes=64, name="of%d%d" % (i, j)) for j in range(2)] for i in range(2)]
+        live = {}
+
+        def run(token, eng):
+            kind = token[:2]
+            ix = [int(c) for c in token[2:]]
+            copy = {"S": nc.scalar.copy, "V": nc.vector.tensor_copy}.get(eng)
+            if kind == "WM":
+                b_ps = ps_one.tile([P, 512], F32, name="acc_one")
+                nc.tensor.matmul(b_ps[:, 0:8], lhsT=bz[:], rhs=ident_bf[:, 0:8], start=True, stop=True)
+                live["b"] = b_ps
+                for g in range(2):
+                    w_ps = ps_two.tile([P, 512], F32, name="acc_two")
+                    nc.tensor.matmul(w_ps[:], lhsT=ones[:], rhs=wz[:, 512 * g : 512 * (g + 1)], start=True, stop=True)
+                    live["w%d" % g] = w_ps
+            elif kind == "WC":
+                copy(out=b_col[:], in_=live["b"][:, 0:8])
+                for g in range(2):
+                    copy(
+                        out=w_bc[:, 512 * g : 512 * (g + 1)].rearrange("p (u r e) -> p u r e", u=2, e=2),
+                        in_=live["w%d" % g][:].rearrange("p (r u e) -> p u r e", u=2, e=2),
+                    )
+            elif kind == "XT":
+                g, u, kg = ix
+                words = x_raw[g][u][:].bitcast(F32)
+                ps = ps_tr.tile([P, 2, 2, P], F32, name="ps_x")
+                for v in range(2):
+                    for e in range(2):
+                        nc.tensor.transpose(ps[:, v, e, :], words[:, e, 256 * kg + v : 256 * (kg + 1) : 2], ident[:])
+                live[token[2:]] = ps
+            elif kind == "XC":
+                g, u, kg = ix
+                c0 = 512 * g + 256 * u
+                copy(
+                    out=xg[:, kg, 4 * c0 : 4 * (c0 + 256)].bitcast(F32).rearrange("p (r e v) -> p r e v", e=2, v=2),
+                    in_=live[token[2:]][:].rearrange("p v e r -> p r e v"),
+                )
+            elif kind == "XQ":
+                g, u, kg = ix
+                c0 = 512 * g + 256 * u
+                nc.vector.quantize_mx(
+                    out=xc[:, kg, c0 : c0 + 256].bitcast(E4M3),
+                    scales=xs[:, kg, c0 : c0 + 256],
+                    in_=xg[:, kg, 4 * c0 : 4 * (c0 + 256)],
+                )
+            elif kind == "AI":
+                m, h, t = ix
+                dst = ag[m][:, 512 * h : 512 * (h + 1), :].rearrange("p (t r) j -> p t r j", t=4)
+                src = a_raw[m][:, :, 512 * h : 512 * (h + 1)].rearrange("p j (r t) -> p t r j", t=4)
+                copy(out=dst[:, 2 * t : 2 * t + 2], in_=src[:, 2 * t : 2 * t + 2])
+            elif kind == "AQ":
+                m, h = ix
+                nc.vector.quantize_mx(
+                    out=ac[m][:, 512 * h : 512 * (h + 1)].bitcast(E4M3),
+                    scales=asc[m][:, 512 * h : 512 * (h + 1)],
+                    in_=ag[m][:, 512 * h : 512 * (h + 1), :].rearrange("p c j -> p (c j)"),
+                )
+            elif kind == "M1":
+                i, g = ix
+                acc = ps_one.tile([P, 512], F32, name="acc_one")
+                for kg in range(2):
+                    nc.tensor.matmul_mx(
+                        out=acc[:],
+                        lhsT=h_sb[:, kg, 256 * i : 256 * (i + 1)].bitcast(E2M1),
+                        lhsT_scale=hs[:, kg, P * i : P * (i + 1)],
+                        rhs=xc[:, kg, 512 * g : 512 * (g + 1)].bitcast(E4M3),
+                        rhs_scale=xs[:, kg, 512 * g : 512 * (g + 1)],
+                        start=(kg == 0),
+                        stop=(kg == 1),
+                    )
+                live["y" + token[2:]] = acc
+            elif kind == "TH":
+                i, g = ix
+                nc.scalar.activation(
+                    out=y[i][:, 512 * g : 512 * (g + 1)], in_=live["y" + token[2:]][:], func=TANH,
+                    bias=b_col[:, i : i + 1], accum_out=sums[:, 2 * i + g : 2 * i + g + 1],
+                )
+            elif kind == "ME":
+                i = ix[0]
+                nc.gpsimd.tensor_scalar(
+                    out=mean[:, i : i + 1], in0=sums[:, 2 * i : 2 * i + 1], scalar1=sums[:, 2 * i + 1 : 2 * i + 2],
+                    scalar2=1.0 / N, op0=ADD, op1=MUL,
+                )
+            elif kind == "ST":
+                i = ix[0]
+                t = et_pool.tile([P, N], BF16, align_bytes=64, name="et_t")
+                nc.vector.scalar_tensor_tensor(
+                    out=t[:], in0=y[i][:], scalar=mean[:, i : i + 1], in1=w_bc[:], op0=SUB, op1=MUL
+                )
+                live["e%d" % i] = t
+            elif kind == "ET":
+                i = ix[0]
+                words = live["e%d" % i][:].bitcast(F32)
+                ps = ps_tr.tile([P, 2, 2, P], F32, name="ps_x")
+                for g in range(2):
+                    for v in range(2):
+                        c = 256 * g + P * v
+                        nc.tensor.transpose(ps[:, g, v, :], words[:, c : c + P], ident[:])
+                live["t%d" % i] = ps
+            elif kind == "EC":
+                i = ix[0]
+                o = P * (i % 2)
+                copy(
+                    out=eg[i // 2][:, :, o : o + P, :].bitcast(F32),
+                    in_=live["t%d" % i][:].rearrange("p g v o -> p g o v"),
+                )
+            elif kind == "EQ":
+                q, g = ix
+                nc.vector.quantize_mx(
+                    out=ec[q][:, g, :].bitcast(E4M3),
+                    scales=es[q][:, g, :],
+                    in_=eg[q][:, g].rearrange("p o j -> p (o j)"),
+                )
+            elif kind == "M2":
+                q, gp, tt = ix
+                acc = ps_two.tile([P, 2, 256], F32, name="acc_two")
+                for s in range(2):
+                    c = 512 * gp + P * (2 * tt + s)
+                    for g in range(2):
+                        nc.tensor.matmul_mx(
+                            out=acc[:, s, :],
+                            lhsT=ac[g][:, c : c + P].bitcast(E4M3),
+                            lhsT_scale=asc[g][:, c : c + P],
+                            rhs=ec[q][:, g, :].bitcast(E4M3),
+                            rhs_scale=es[q][:, g, :],
+                            start=(g == 0),
+                            stop=(g == 1),
+                        )
+                live["p" + token[2:]] = acc
+            elif kind == "PC":
+                plain = og_pool.tile([P, 2, 256], F32, align_bytes=64, name="plain")
+                nc.scalar.copy(out=plain[:], in_=live["p" + token[2:]][:])
+                live["p" + token[2:]] = plain
+            elif kind == "TT":
+                q, gp, tt = ix
+                c = 256 * (q % 2)
+                engine = nc.gpsimd if eng == "G" else nc.vector
+                engine.tensor_tensor(
+                    out=of[q // 2][gp][:, 2 * tt : 2 * tt + 2, c : c + 256], in0=live["p" + token[2:]][:],
+                    in1=rho_sb[gp][:, 2 * tt : 2 * tt + 2, 256 * q : 256 * (q + 1)], op=MUL,
+                )
+            elif kind == "GR":
+                q, gp, c = ix
+                if token[2:4] not in live:
+                    live[token[2:4]] = og_pool.tile([P, 256, 4], BF16, align_bytes=64, name="og")
+                dst = live[token[2:4]][:, P * c : P * (c + 1), :]
+                c1 = 256 * (q % 2) + P * c
+                src = of[q // 2][gp][:, :, c1 : c1 + P].rearrange("p t o -> p o t")
+                if eng == "G":
+                    nc.gpsimd.tensor_scalar(out=dst, in0=src, scalar1=1.0, scalar2=-0.0, op0=MUL, op1=ADD)
+                else:
+                    copy(out=dst, in_=src)
+            elif kind == "OQ":
+                q, gp = ix
+                if "c%d" % q not in live:
+                    live["c%d" % q] = og_pool.tile([P, 2, 256], U32, align_bytes=64, name="oc")
+                t = live["c%d" % q]
+                c = 256 * (q % 2)
+                nc.vector.quantize_mx(
+                    out=t[:, gp, :].bitcast(E4M3),
+                    scales=osc[q // 2][:, gp, c : c + 256],
+                    in_=live[token[2:4]][:].rearrange("p o t -> p (o t)"),
+                )
+            elif kind == "SC":
+                q = ix[0]
+                dst = out_1.rearrange("g p m t -> p g (m t)")[:, :, 1024 * q : 1024 * (q + 1)]
+                nc.sync.dma_start(out=dst.bitcast(I32), in_=live["c%d" % q][:].bitcast(I32))
+            elif kind == "SF":
+                q, gp = ix
+                c0 = 512 * (q // 2) if q < 2 else 256 * q
+                c1 = 256 * (q + 1)
+                dst = out_0[512 * gp : 512 * (gp + 1), c0:c1].rearrange("(p t) o -> p t o", t=4)
+                nc.sync.dma_start(out=dst, in_=of[q // 2][gp][:, :, c0 - 512 * (q // 2) : c1 - 512 * (q // 2)])
+            elif kind == "SS":
+                hh = ix[0]
+                for q in range(4):
+                    dst = out_2[:, 4 * q : 4 * q + 4, 512 * hh : 512 * (hh + 1)].bitcast(I32).rearrange("g q m -> q g m")
+                    queue = nc.scalar if (q % 2 and hh == 1) else nc.sync
+                    queue.dma_start(out=dst, in_=osc[hh][32 * q : 32 * q + 4, :, :].bitcast(I32))
+            else:
+                raise ValueError(token)
+
+        for item in ORDER.split():
+            token, eng = item.split(".")
+            run(mark(token), eng)

@@ -79,8 +79,8 @@ def tile_localisedweightedcrossmoment_kernel(tc, x, h_words, h_scales, b, a, w, 
         def load_h():
             nc.sync.dma_start(out=h_sb[:].bitcast(I32), in_=h_words.bitcast(I32).rearrange("g p c -> p g c"))
 
-        def load_hs(queue):
-            for q in range(4):
+        def load_hs(queue, qs=range(4)):
+            for q in qs:
                 queue.dma_start(
                     out=hs[32 * q : 32 * q + 4, :, :].bitcast(I32),
                     in_=h_scales.bitcast(I32)[:, 4 * q : 4 * q + 4, :].rearrange("g q n -> q g n"),
@@ -90,12 +90,13 @@ def tile_localisedweightedcrossmoment_kernel(tc, x, h_words, h_scales, b, a, w, 
             queue.dma_start(out=wz[0:1, :], in_=w.rearrange("(r n) -> r n", r=1))
             queue.dma_start(out=bz[0:8, :], in_=b.rearrange("(c p) -> c p", p=P))
 
-        load_wb(nc.gpsimd)
+        load_wb(nc.scalar)
         load_x(0, 0)
         load_x(0, 1)
-        load_hs(nc.sync)
+        load_hs(nc.sync, (0, 1, 2))
         load_h()
         load_rows(a_raw, a, 0)
+        load_hs(nc.sync, (3,))
         load_x(1, 0)
         load_x(1, 1)
         load_rows(a_raw, a, 1)

@@ -21,19 +21,18 @@ FLOPS = 2 * 2 * N * N * N
 
 
 ORDER = """
-XT001.P XT000.P XC001.V WM.P XC000.S XQ001.V XT010.P XQ000.V WC.S XT011.P XC010.V XC011.V XQ010.V XQ011.V
-M100.P AI001.V AI011.S M140.P AI010.V M110.P TH00.S AI000.V XT100.P TH40.S AQ01.V XT101.P XC100.S AQ00.V
-M130.P XC101.S XQ100.V XT110.P TH30.S XQ101.V XT111.P XC110.V TH10.S M120.P XC111.V AI110.S M160.P AI101.V
-M170.P XQ110.V TH60.S XQ111.V AI111.V TH70.S M121.P AI100.V TH20.S M101.P AQ11.V TH21.S M111.P AQ10.V TH01.S
-M171.P ME2.G ST2.V TH11.S M141.P ME0.G TH71.S M131.P ME1.G ST0.V TH41.S ET2.P ME7.G M151.P TH31.S ST1.V ME4.G
-ET0.P EC2.S ME3.G M161.P ST3.V EC0.S ET1.P TH61.S M150.P ST7.V EC1.S ME6.G ET3.P TH50.S EQ01.V ET7.P EQ00.V
-EC3.S ST4.V M2001.P EC7.S M2011.P TH51.S EQ11.V M2000.P EQ10.V PC011.S ME5.G TT001.V ET4.P ST5.V M2111.P EC4.S
-M2100.P PC111.S TT000.V TT011.G ET5.P TT100.V GR001.S M2101.P EC5.V TT111.G GR000.S M2010.P TT101.V M2110.P
-TT010.V GR101.S SF10.D EQ20.V GR100.S OQ00.V EQ21.V GR011.S OQ10.V M2211.P TT110.V GR010.S M2201.P ST6.V
-SF11.D PC211.S M2210.P GR110.S M2200.P TT210.V TT211.G GR111.S ET6.P TT201.V EC6.S OQ11.V SF21.D GR210.V SC1.D
-EQ30.V EQ31.V OQ01.V M2301.P TT200.V GR211.G SC0.D SS0.D M2311.P TT301.V GR200.S SF20.D M2310.P GR201.V
-TT311.V M2300.P TT310.V TT300.V GR310.G SF31.D GR301.S SF30.D GR311.V GR300.G OQ31.V OQ30.V OQ20.V SC3.D
-OQ21.V SC2.D SS1.D
+XT001.P XT000.P XC001.S BM.P XC000.S XQ001.V XT011.P BC.S XQ000.V XT010.P XC011.V WM.P XC010.S XQ011.V XQ010.V
+WC.S M150.P M110.P AI011.V TH50.S M140.P AI000.V TH10.S XT100.P AI010.V TH40.S XT101.P AI001.V XC100.S M100.P
+AQ01.V XC101.S XT110.P AQ00.V TH00.S XQ100.V XT111.P XQ101.V XC110.S M130.P AI100.V XC111.S M120.P XQ110.V
+TH30.S XQ111.V AI101.V M121.P TH20.S AI110.V M131.P TH21.S M141.P AQ10.V TH31.S ME2.G M101.P ST2.V TH41.S
+ME3.G M161.P TH01.S ME4.G M111.P ST3.V TH61.S ET2.P ME0.G M170.P TH11.S ST4.V EC2.S ET3.P ME1.G M171.P ST1.V
+EC3.S ET4.P TH71.S EQ11.V ET1.P EQ10.V TH70.S M160.P ST0.V EC4.S M2100.P ME7.G TH60.S ST7.V ET0.P EC1.S
+M2101.P ME6.G TT100.V EC0.S ET7.P TT101.V AI111.S M151.P EQ00.V EQ01.V ST6.V GR100.S M2000.P TH51.S M2001.P
+AQ11.V ET6.P EC7.S ME5.G TT001.V M2111.P EC6.S TT000.V GR101.S M2110.P TT111.V SF00.D M2010.P GR000.S TT110.V
+M2011.P GR001.S TT010.V GR111.S TT011.V GR110.S OQ10.V SF01.D ST5.V GR010.S GR011.S OQ11.V ET5.P OQ00.V EQ31.V
+SD00.D EC5.S EQ30.V OQ01.V M2310.P EQ21.V SD01.D SS0.D EQ20.V M2311.P TT310.V M2200.P TT311.V M2211.P TT200.V
+GR310.S SG3.D M2300.P TT211.V GR311.S M2210.P TT300.V M2301.P TT210.V M2201.P TT301.V GR210.S SG2.D TT201.V
+GR211.S OQ31.V SF10.D GR201.S OQ21.V SD11.D GR300.S GR301.S GR200.S OQ30.V OQ20.V SD10.D SS1.D
 """
 
 
@@ -86,17 +85,19 @@ def tile_localisedweightedcrossmoment_kernel(tc, x, h_words, h_scales, b, a, w, 
                     in_=h_scales.bitcast(I32)[:, 4 * q : 4 * q + 4, :].rearrange("g q n -> q g n"),
                 )
 
-        def load_wb(queue):
+        def load_w(queue):
             queue.dma_start(out=wz[0:1, :], in_=w.rearrange("(r n) -> r n", r=1))
+
+        def load_b(queue):
             queue.dma_start(out=bz[0:8, :], in_=b.rearrange("(c p) -> c p", p=P))
 
-        load_wb(nc.scalar)
         load_x(0, 0)
         load_x(0, 1)
-        load_hs(nc.sync, (0, 1, 2))
         load_h()
+        load_hs(nc.scalar)
+        load_b(nc.scalar)
+        load_w(nc.gpsimd)
         load_rows(a_raw, a, 0)
-        load_hs(nc.sync, (3,))
         load_x(1, 0)
         load_x(1, 1)
         load_rows(a_raw, a, 1)
@@ -128,16 +129,16 @@ def tile_localisedweightedcrossmoment_kernel(tc, x, h_words, h_scales, b, a, w, 
             kind = token[:2]
             ix = [int(c) for c in token[2:]]
             copy = {"S": nc.scalar.copy, "V": nc.vector.tensor_copy}.get(eng)
-            if kind == "WM":
-                b_ps = ps_one.tile([P, 512], F32, name="acc_one")
-                nc.tensor.matmul(b_ps[:, 0:8], lhsT=bz[:], rhs=ident_bf[:, 0:8], start=True, stop=True)
-                live["b"] = b_ps
+            if kind == "BM":
+                live["b"] = ps_one.tile([P, 512], F32, name="acc_one")
+                nc.tensor.matmul(live["b"][:, 0:8], lhsT=bz[:], rhs=ident_bf[:, 0:8], start=True, stop=True)
+            elif kind == "BC":
+                nc.scalar.copy(out=b_col[:], in_=live["b"][:, 0:8])
+            elif kind == "WM":
                 for g in range(2):
-                    w_ps = ps_two.tile([P, 512], F32, name="acc_two")
-                    nc.tensor.matmul(w_ps[:], lhsT=ones[:], rhs=wz[:, 512 * g : 512 * (g + 1)], start=True, stop=True)
-                    live["w%d" % g] = w_ps
+                    live["w%d" % g] = ps_two.tile([P, 512], F32, name="acc_two")
+                    nc.tensor.matmul(live["w%d" % g][:], lhsT=ones[:], rhs=wz[:, 512 * g : 512 * (g + 1)], start=True, stop=True)
             elif kind == "WC":
-                copy(out=b_col[:], in_=live["b"][:, 0:8])
                 for g in range(2):
                     copy(
                         out=w_bc[:, 512 * g : 512 * (g + 1)].rearrange("p (u r e) -> p u r e", u=2, e=2),
@@ -275,25 +276,24 @@ def tile_localisedweightedcrossmoment_kernel(tc, x, h_words, h_scales, b, a, w, 
                     copy(out=dst, in_=src)
             elif kind == "OQ":
                 q, gp = ix
-                if "c%d" % q not in live:
-                    live["c%d" % q] = og_pool.tile([P, 2, 256], U32, align_bytes=64, name="oc")
-                t = live["c%d" % q]
+                key = "c%d%d" % (q // 2, gp)
+                if key not in live:
+                    live[key] = keep.tile([P, 512], U32, align_bytes=64, name="o" + key)
                 c = 256 * (q % 2)
                 nc.vector.quantize_mx(
-                    out=t[:, gp, :].bitcast(E4M3),
+                    out=live[key][:, c : c + 256].bitcast(E4M3),
                     scales=osc[q // 2][:, gp, c : c + 256],
                     in_=live[token[2:4]][:].rearrange("p o t -> p (o t)"),
                 )
-            elif kind == "SC":
-                q = ix[0]
-                dst = out_1.rearrange("g p m t -> p g (m t)")[:, :, 1024 * q : 1024 * (q + 1)]
-                nc.sync.dma_start(out=dst.bitcast(I32), in_=live["c%d" % q][:].bitcast(I32))
-            elif kind == "SF":
-                q, gp = ix
-                c0 = 512 * (q // 2) if q < 2 else 256 * q
-                c1 = 256 * (q + 1)
-                dst = out_0[512 * gp : 512 * (gp + 1), c0:c1].rearrange("(p t) o -> p t o", t=4)
-                nc.sync.dma_start(out=dst, in_=of[q // 2][gp][:, :, c0 - 512 * (q // 2) : c1 - 512 * (q // 2)])
+            elif kind == "SD":
+                hh, gp = ix
+                dst = out_1[gp].rearrange("p m t -> p (m t)")[:, 2048 * hh : 2048 * (hh + 1)]
+                nc.sync.dma_start(out=dst.bitcast(I32), in_=live["c%d%d" % (hh, gp)][:].bitcast(I32))
+            elif kind in ("SF", "SG"):
+                hh, gp = ix if kind == "SF" else (1, 1)
+                c0, c1 = (0, 512) if kind == "SF" else (256 * (ix[0] - 2), 256 * (ix[0] - 1))
+                dst = out_0[512 * gp : 512 * (gp + 1), 512 * hh + c0 : 512 * hh + c1].rearrange("(p t) o -> p t o", t=4)
+                nc.sync.dma_start(out=dst, in_=of[hh][gp][:, :, c0:c1])
             elif kind == "SS":
                 hh = ix[0]
                 for q in range(4):

@@ -21,18 +21,19 @@ FLOPS = 2 * 2 * N * N * N
 
 
 ORDER = """
-XT001.P XT000.P XC001.S BM.P XC000.S XQ001.V XT011.P BC.S XQ000.V XT010.P XC011.V WM.P XC010.S XQ011.V XQ010.V
-WC.S M150.P M110.P AI011.V TH50.S M140.P AI000.V TH10.S XT100.P AI010.V TH40.S XT101.P AI001.V XC100.S M100.P
-AQ01.V XC101.S XT110.P AQ00.V TH00.S XQ100.V XT111.P XQ101.V XC110.S M130.P AI100.V XC111.S M120.P XQ110.V
-TH30.S XQ111.V AI101.V M121.P TH20.S AI110.V M131.P TH21.S M141.P AQ10.V TH31.S ME2.G M101.P ST2.V TH41.S
-ME3.G M161.P TH01.S ME4.G M111.P ST3.V TH61.S ET2.P ME0.G M170.P TH11.S ST4.V EC2.S ET3.P ME1.G M171.P ST1.V
-EC3.S ET4.P TH71.S EQ11.V ET1.P EQ10.V TH70.S M160.P ST0.V EC4.S M2100.P ME7.G TH60.S ST7.V ET0.P EC1.S
-M2101.P ME6.G TT100.V EC0.S ET7.P TT101.V AI111.S M151.P EQ00.V EQ01.V ST6.V GR100.S M2000.P TH51.S M2001.P
-AQ11.V ET6.P EC7.S ME5.G TT001.V M2111.P EC6.S TT000.V GR101.S M2110.P TT111.V SF00.D M2010.P GR000.S TT110.V
-M2011.P GR001.S TT010.V GR111.S TT011.V GR110.S OQ10.V SF01.D ST5.V GR010.S GR011.S OQ11.V ET5.P OQ00.V EQ31.V
-SD00.D EC5.S EQ30.V OQ01.V M2310.P EQ21.V SD01.D SS0.D EQ20.V M2311.P TT310.V M2200.P TT311.V M2211.P TT200.V
-GR310.S SG3.D M2300.P TT211.V GR311.S M2210.P TT300.V M2301.P TT210.V M2201.P TT301.V GR210.S SG2.D TT201.V
-GR211.S OQ31.V SF10.D GR201.S OQ21.V SD11.D GR300.S GR301.S GR200.S OQ30.V OQ20.V SD10.D SS1.D
+XT000.P XC000.V XT001.P XT011.P XQ000.V XC001.S WM.P XT010.P XQ001.V BM.P WC.V XC011.S XQ011.V XT100.P XC010.S
+AI001.S XC100.S XT101.P BC.S AI000.V XQ010.V AI011.V M130.P M100.P AI010.V XT110.P XC101.S AQ00.V XT111.P
+M110.P XQ101.V XQ100.V AQ01.V TH30.S AI110.V TH00.S AI101.V M150.P XC110.S XQ110.V XC111.S TH10.S M120.P
+XQ111.V M101.P TH50.S AI100.V AI111.V M111.P TH20.S M140.P TH01.S TH11.S TH40.S M121.P ME0.G TH21.S M131.P
+ME1.G AQ10.V M141.P M151.P AQ11.V TH31.S ME2.G ST0.V TH41.S ST1.V ET0.P ME3.G TH51.S ET1.P M171.P M161.P
+M160.P EC1.S ST2.V ST3.V EC0.S ME4.G EQ00.V EQ01.V ST4.V TH71.S ME5.G TH61.S ET3.P ET2.P EC2.S M2010.P M2001.P
+EC3.S M2000.P ET4.P ST5.V EQ10.V TT010.V TH60.S EQ11.V M170.P EC4.S TT000.V M2100.P ME6.G M2101.P TT001.V
+M2110.P TT100.V TH70.S ET5.P TT101.V M2111.P EC5.S ST6.V TT110.V M2011.P ME7.G ET6.P TT111.V GR001.S GR100.S
+TT011.V SF00.D ST7.V ET7.P EQ21.V GR000.S GR101.S EQ20.V OQ00.V M2200.P OQ10.V M2201.P GR111.S EC6.S EC7.S
+M2211.P GR010.S TT200.V SF01.D TT201.V EQ30.V TT211.V M2210.P GR110.S TT210.V SD00.D EQ31.V GR011.S OQ11.V
+GR201.S M2300.P OQ01.V SG20.D GR211.V SG21.D M2301.P SD01.D TT300.V M2311.P TT301.V GR300.S GR200.S TT311.V
+GR210.S M2310.P TT310.V SS0.D SG30.D GR301.V OQ21.V GR310.S OQ20.V GR311.S OQ30.V SG31.D OQ31.V SD10.D SS1.D
+SD11.D
 """
 
 
@@ -169,9 +170,9 @@ def tile_localisedweightedcrossmoment_kernel(tc, x, h_words, h_scales, b, a, w, 
                 )
             elif kind == "AI":
                 m, h, t = ix
-                dst = ag[m][:, 512 * h : 512 * (h + 1), :].rearrange("p (t r) j -> p t r j", t=4)
-                src = a_raw[m][:, :, 512 * h : 512 * (h + 1)].rearrange("p j (r t) -> p t r j", t=4)
-                copy(out=dst[:, 2 * t : 2 * t + 2], in_=src[:, 2 * t : 2 * t + 2])
+                dst = ag[m][:, 512 * h : 512 * (h + 1), :].rearrange("p (t r) j -> p r j t", t=4)
+                src = a_raw[m][:, :, 512 * h : 512 * (h + 1)].rearrange("p j (r t) -> p r j t", t=4)
+                copy(out=dst[:, 64 * t : 64 * t + 64], in_=src[:, 64 * t : 64 * t + 64])
             elif kind == "AQ":
                 m, h = ix
                 nc.vector.quantize_mx(
@@ -269,7 +270,8 @@ def tile_localisedweightedcrossmoment_kernel(tc, x, h_words, h_scales, b, a, w, 
                     live[token[2:4]] = og_pool.tile([P, 256, 4], BF16, align_bytes=64, name="og")
                 dst = live[token[2:4]][:, P * c : P * (c + 1), :]
                 c1 = 256 * (q % 2) + P * c
-                src = of[q // 2][gp][:, :, c1 : c1 + P].rearrange("p t o -> p o t")
+                src = of[q // 2][gp][:, :, c1 : c1 + P].rearrange("p t (c i) -> p c t i", i=4)
+                dst = dst.rearrange("p (c i) t -> p c t i", i=4)
                 if eng == "G":
                     nc.gpsimd.tensor_scalar(out=dst, in0=src, scalar1=1.0, scalar2=-0.0, op0=MUL, op1=ADD)
                 else:
@@ -290,7 +292,7 @@ def tile_localisedweightedcrossmoment_kernel(tc, x, h_words, h_scales, b, a, w, 
                 dst = out_1[gp].rearrange("p m t -> p (m t)")[:, 2048 * hh : 2048 * (hh + 1)]
                 nc.sync.dma_start(out=dst.bitcast(I32), in_=live["c%d%d" % (hh, gp)][:].bitcast(I32))
             elif kind in ("SF", "SG"):
-                hh, gp = ix if kind == "SF" else (1, 1)
+                hh, gp = ix[0] if kind == "SF" else 1, ix[1]
                 c0, c1 = (0, 512) if kind == "SF" else (256 * (ix[0] - 2), 256 * (ix[0] - 1))
                 dst = out_0[512 * gp : 512 * (gp + 1), 512 * hh + c0 : 512 * hh + c1].rearrange("(p t) o -> p t o", t=4)
                 nc.sync.dma_start(out=dst, in_=of[hh][gp][:, :, c0:c1])

from contextlib import ExitStack

import concourse.mybir as mybir
from concourse.masks import make_identity

F32 = mybir.dt.float32
BF16 = mybir.dt.bfloat16
I32 = mybir.dt.int32
U32 = mybir.dt.uint32
U8 = mybir.dt.uint8
E4M3 = mybir.dt.float8_e4m3fn_x4
E2M1 = mybir.dt.float4_e2m1fn_x4
TANH = mybir.ActivationFunctionType.Tanh
ADD = mybir.AluOpType.add
SUB = mybir.AluOpType.subtract
MUL = mybir.AluOpType.mult

P = 128
N = 1024
FLOPS = 2 * 2 * N * N * N


ORDER = """
XT000.P XC000.V XT001.P XT011.P XQ000.V XC001.S WM.P XT010.P XQ001.V BM.P WC.V XC011.S XQ011.V XT100.P XC010.S
AI001.S XC100.S XT101.P BC.S AI000.V XQ010.V AI011.V M130.P M100.P AI010.V XT110.P XC101.S AQ00.V XT111.P
M110.P XQ101.V XQ100.V AQ01.V TH30.S AI110.V TH00.S AI101.V M150.P XC110.S XQ110.V XC111.S TH10.S M120.P
XQ111.V M101.P TH50.S AI100.V AI111.V M111.P TH20.S M140.P TH01.S TH11.S TH40.S M121.P ME0.G TH21.S M131.P
ME1.G AQ10.V M141.P M151.P AQ11.V TH31.S ME2.G ST0.V TH41.S ST1.V ET0.P ME3.G TH51.S ET1.P M171.P M161.P
M160.P EC1.S ST2.V ST3.V EC0.S ME4.G EQ00.V EQ01.V ST4.V TH71.S ME5.G TH61.S ET3.P ET2.P EC2.S M2010.P M2001.P
EC3.S M2000.P ET4.P ST5.V EQ10.V TT010.V TH60.S EQ11.V M170.P EC4.S TT000.V M2100.P ME6.G M2101.P TT001.V
M2110.P TT100.V TH70.S ET5.P TT101.V M2111.P EC5.S ST6.V TT110.V M2011.P ME7.G ET6.P TT111.V GR001.S GR100.S
TT011.V SF00.D ST7.V ET7.P EQ21.V GR000.S GR101.S EQ20.V OQ00.V M2200.P OQ10.V M2201.P GR111.S EC6.S EC7.S
M2211.P GR010.S TT200.V SF01.D TT201.V EQ30.V TT211.V M2210.P GR110.S TT210.V SD00.D EQ31.V GR011.S OQ11.V
GR201.S M2300.P OQ01.V SG20.D GR211.V SG21.D M2301.P SD01.D TT300.V M2311.P TT301.V GR300.S GR200.S TT311.V
GR210.S M2310.P TT310.V SS0.D SG30.D GR301.V OQ21.V GR310.S OQ20.V GR311.S OQ30.V SG31.D OQ31.V SD10.D SS1.D
SD11.D
"""


def mark(token):
    return token


def tile_localisedweightedcrossmoment_kernel(tc, x, h_words, h_scales, b, a, w, rho, out_0, out_1, out_2):
    nc = tc.nc
    with ExitStack() as ctx:
        ctx.enter_context(tc.manual_schedule())
        keep = ctx.enter_context(tc.tile_pool(name="keep", bufs=1))
        et_pool = ctx.enter_context(tc.tile_pool(name="et_pool", bufs=3))
        og_pool = ctx.enter_context(tc.tile_pool(name="og_pool", bufs=4))
        ps_tr = ctx.enter_context(tc.psum_pool(name="ps_tr", bufs=2))
        ps_one = ctx.enter_context(tc.psum_pool(name="ps_one", bufs=3))
        ps_two = ctx.enter_context(tc.psum_pool(name="ps_two", bufs=3))

        ident = keep.tile([P, P], F32, align_bytes=64, name="ident")
        make_identity(nc, ident[:])
        hs = keep.tile([P, 2, N], U8, align_bytes=64, name="hs")
        wz = keep.tile([P, N], BF16, align_bytes=64, name="wz")
        bz = keep.tile([P, P], BF16, align_bytes=64, name="bz")
        ones = keep.tile([P, P], BF16, align_bytes=64, name="ones")
        nc.vector.memset(hs[:].bitcast(I32), 0)
        nc.vector.memset(wz[:].bitcast(I32), 0)
        nc.vector.memset(bz[:].bitcast(I32), 0)
        nc.gpsimd.memset(ones[:], 1.0)
        ident_bf = keep.tile([P, P], BF16, align_bytes=64, name="ident_bf")

        x_raw = [[keep.tile([P, 2, N], BF16, align_bytes=64, name="x_raw%d%d" % (g, u)) for u in range(2)] for g in range(2)]
        a_raw = [keep.tile([P, 4, N], BF16, align_bytes=64, name="a_raw%d" % g) for g in range(2)]
        rho_sb = [keep.tile([P, 4, N], BF16, align_bytes=64, name="rho_sb%d" % g) for g in range(2)]
        h_sb = keep.tile([P, 2, 2 * N], U8, align_bytes=64, name="h_sb")

        def load_x(g, u):
            src = x[512 * g : 512 * (g + 1), :].rearrange("(p j) d -> p j d", j=4)
            nc.sync.dma_start(out=x_raw[g][u][:], in_=src[:, 2 * u : 2 * u + 2, :])

        def load_rows(dst, src, g):
            nc.sync.dma_start(out=dst[g][:], in_=src[512 * g : 512 * (g + 1), :].rearrange("(p j) d -> p j d", j=4))

        def load_h():
            nc.sync.dma_start(out=h_sb[:].bitcast(I32), in_=h_words.bitcast(I32).rearrange("g p c -> p g c"))

        def load_hs(queue, qs=range(4)):
            for q in qs:
                queue.dma_start(
                    out=hs[32 * q : 32 * q + 4, :, :].bitcast(I32),
                    in_=h_scales.bitcast(I32)[:, 4 * q : 4 * q + 4, :].rearrange("g q n -> q g n"),
                )

        def load_w(queue):
            queue.dma_start(out=wz[0:1, :], in_=w.rearrange("(r n) -> r n", r=1))

        def load_b(queue):
            queue.dma_start(out=bz[0:8, :], in_=b.rearrange("(c p) -> c p", p=P))

        load_x(0, 0)
        load_x(0, 1)
        load_h()
        load_hs(nc.scalar)
        load_b(nc.scalar)
        load_w(nc.gpsimd)
        load_rows(a_raw, a, 0)
        load_x(1, 0)
        load_x(1, 1)
        load_rows(a_raw, a, 1)
        load_rows(rho_sb, rho, 0)
        load_rows(rho_sb, rho, 1)
        warm = keep.tile([P, 1], F32, name="warm")
        nc.scalar.activation(out=warm[:], in_=ident[:, 0:1], func=TANH)
        nc.vector.tensor_copy(out=ident_bf[:], in_=ident[:])

        xg = keep.tile([P, 2, 4 * N], BF16, align_bytes=64, name="xg")
        xc = keep.tile([P, 2, N], U32, align_bytes=64, name="xc")
        xs = keep.tile([P, 2, N], U8, align_bytes=64, name="xs")
        ag = [keep.tile([P, N, 4], BF16, align_bytes=64, name="ag%d" % g) for g in range(2)]
        ac = [keep.tile([P, N], U32, align_bytes=64, name="ac%d" % g) for g in range(2)]
        asc = [keep.tile([P, N], U8, align_bytes=64, name="asc%d" % g) for g in range(2)]
        b_col = keep.tile([P, 8], F32, name="b_col")
        w_bc = keep.tile([P, N], BF16, align_bytes=64, name="w_bc")
        y = [keep.tile([P, N], F32, align_bytes=64, name="y%d" % i) for i in range(8)]
        sums = keep.tile([P, 16], F32, name="sums")
        mean = keep.tile([P, 8], F32, name="mean")
        eg = [keep.tile([P, 2, 256, 4], BF16, align_bytes=64, name="eg%d" % i) for i in range(4)]
        ec = [keep.tile([P, 2, 256], U32, align_bytes=64, name="ec%d" % i) for i in range(4)]
        es = [keep.tile([P, 2, 256], U8, align_bytes=64, name="es%d" % i) for i in range(4)]
        osc = [keep.tile([P, 2, 512], U8, align_bytes=64, name="osc%d" % i) for i in range(2)]
        of = [[keep.tile([P, 4, 512], F32, align_bytes=64, name="of%d%d" % (i, j)) for j in range(2)] for i in range(2)]
        live = {}

        def run(token, eng):
            kind = token[:2]
            ix = [int(c) for c in token[2:]]
            copy = {"S": nc.scalar.copy, "V": nc.vector.tensor_copy}.get(eng)
            if kind == "BM":
                live["b"] = ps_one.tile([P, 512], F32, name="acc_one")
                nc.tensor.matmul(live["b"][:, 0:8], lhsT=bz[:], rhs=ident_bf[:, 0:8], start=True, stop=True)
            elif kind == "BC":
                nc.scalar.copy(out=b_col[:], in_=live["b"][:, 0:8])
            elif kind == "WM":
                for g in range(2):
                    live["w%d" % g] = ps_two.tile([P, 512], F32, name="acc_two")
                    nc.tensor.matmul(live["w%d" % g][:], lhsT=ones[:], rhs=wz[:, 512 * g : 512 * (g + 1)], start=True, stop=True)
            elif kind == "WC":
                for g in range(2):
                    copy(
                        out=w_bc[:, 512 * g : 512 * (g + 1)].rearrange("p (u r e) -> p u r e", u=2, e=2),
                        in_=live["w%d" % g][:].rearrange("p (r u e) -> p u r e", u=2, e=2),
                    )
            elif kind == "XT":
                g, u, kg = ix
                words = x_raw[g][u][:].bitcast(F32)
                ps = ps_tr.tile([P, 2, 2, P], F32, name="ps_x")
                for v in range(2):
                    for e in range(2):
                        nc.tensor.transpose(ps[:, v, e, :], words[:, e, 256 * kg + v : 256 * (kg + 1) : 2], ident[:])
                live[token[2:]] = ps
            elif kind == "XC":
                g, u, kg = ix
                c0 = 512 * g + 256 * u
                copy(
                    out=xg[:, kg, 4 * c0 : 4 * (c0 + 256)].bitcast(F32).rearrange("p (r e v) -> p r e v", e=2, v=2),
                    in_=live[token[2:]][:].rearrange("p v e r -> p r e v"),
                )
            elif kind == "XQ":
                g, u, kg = ix
                c0 = 512 * g + 256 * u
                nc.vector.quantize_mx(
                    out=xc[:, kg, c0 : c0 + 256].bitcast(E4M3),
                    scales=xs[:, kg, c0 : c0 + 256],
                    in_=xg[:, kg, 4 * c0 : 4 * (c0 + 256)],
                )
            elif kind == "AI":
                m, h, t = ix
                dst = ag[m][:, 512 * h : 512 * (h + 1), :].rearrange("p (t r) j -> p r j t", t=4)
                src = a_raw[m][:, :, 512 * h : 512 * (h + 1)].rearrange("p j (r t) -> p r j t", t=4)
                copy(out=dst[:, 64 * t : 64 * t + 64], in_=src[:, 64 * t : 64 * t + 64])
            elif kind == "AQ":
                m, h = ix
                nc.vector.quantize_mx(
                    out=ac[m][:, 512 * h : 512 * (h + 1)].bitcast(E4M3),
                    scales=asc[m][:, 512 * h : 512 * (h + 1)],
                    in_=ag[m][:, 512 * h : 512 * (h + 1), :].rearrange("p c j -> p (c j)"),
                )
            elif kind == "M1":
                i, g = ix
                acc = ps_one.tile([P, 512], F32, name="acc_one")
                for kg in range(2):
                    nc.tensor.matmul_mx(
                        out=acc[:],
                        lhsT=h_sb[:, kg, 256 * i : 256 * (i + 1)].bitcast(E2M1),
                        lhsT_scale=hs[:, kg, P * i : P * (i + 1)],
                        rhs=xc[:, kg, 512 * g : 512 * (g + 1)].bitcast(E4M3),
                        rhs_scale=xs[:, kg, 512 * g : 512 * (g + 1)],
                        start=(kg == 0),
                        stop=(kg == 1),
                    )
                live["y" + token[2:]] = acc
            elif kind == "TH":
                i, g = ix
                nc.scalar.activation(
                    out=y[i][:, 512 * g : 512 * (g + 1)], in_=live["y" + token[2:]][:], func=TANH,
                    bias=b_col[:, i : i + 1], accum_out=sums[:, 2 * i + g : 2 * i + g + 1],
                )
            elif kind == "ME":
                i = ix[0]
                nc.gpsimd.tensor_scalar(
                    out=mean[:, i : i + 1], in0=sums[:, 2 * i : 2 * i + 1], scalar1=sums[:, 2 * i + 1 : 2 * i + 2],
                    scalar2=1.0 / N, op0=ADD, op1=MUL,
                )
            elif kind == "ST":
                i = ix[0]
                t = et_pool.tile([P, N], BF16, align_bytes=64, name="et_t")
                nc.vector.scalar_tensor_tensor(
                    out=t[:], in0=y[i][:], scalar=mean[:, i : i + 1], in1=w_bc[:], op0=SUB, op1=MUL
                )
                live["e%d" % i] = t
            elif kind == "ET":
                i = ix[0]
                words = live["e%d" % i][:].bitcast(F32)
                ps = ps_tr.tile([P, 2, 2, P], F32, name="ps_x")
                for g in range(2):
                    for v in range(2):
                        c = 256 * g + P * v
                        nc.tensor.transpose(ps[:, g, v, :], words[:, c : c + P], ident[:])
                live["t%d" % i] = ps
            elif kind == "EC":
                i = ix[0]
                o = P * (i % 2)
                copy(
                    out=eg[i // 2][:, :, o : o + P, :].bitcast(F32),
                    in_=live["t%d" % i][:].rearrange("p g v o -> p g o v"),
                )
            elif kind == "EQ":
                q, g = ix
                nc.vector.quantize_mx(
                    out=ec[q][:, g, :].bitcast(E4M3),
                    scales=es[q][:, g, :],
                    in_=eg[q][:, g].rearrange("p o j -> p (o j)"),
                )
            elif kind == "M2":
                q, gp, tt = ix
                acc = ps_two.tile([P, 2, 256], F32, name="acc_two")
                for s in range(2):
                    c = 512 * gp + P * (2 * tt + s)
                    for g in range(2):
                        nc.tensor.matmul_mx(
                            out=acc[:, s, :],
                            lhsT=ac[g][:, c : c + P].bitcast(E4M3),
                            lhsT_scale=asc[g][:, c : c + P],
                            rhs=ec[q][:, g, :].bitcast(E4M3),
                            rhs_scale=es[q][:, g, :],
                            start=(g == 0),
                            stop=(g == 1),
                        )
                live["p" + token[2:]] = acc
            elif kind == "PC":
                plain = og_pool.tile([P, 2, 256], F32, align_bytes=64, name="plain")
                nc.scalar.copy(out=plain[:], in_=live["p" + token[2:]][:])
                live["p" + token[2:]] = plain
            elif kind == "TT":
                q, gp, tt = ix
                c = 256 * (q % 2)
                engine = nc.gpsimd if eng == "G" else nc.vector
                engine.tensor_tensor(
                    out=of[q // 2][gp][:, 2 * tt : 2 * tt + 2, c : c + 256], in0=live["p" + token[2:]][:],
                    in1=rho_sb[gp][:, 2 * tt : 2 * tt + 2, 256 * q : 256 * (q + 1)], op=MUL,
                )
            elif kind == "GR":
                q, gp, c = ix
                if token[2:4] not in live:
                    live[token[2:4]] = og_pool.tile([P, 256, 4], BF16, align_bytes=64, name="og")
                dst = live[token[2:4]][:, P * c : P * (c + 1), :]
                c1 = 256 * (q % 2) + P * c
                src = of[q // 2][gp][:, :, c1 : c1 + P].rearrange("p t (c i) -> p c t i", i=4)
                dst = dst.rearrange("p (c i) t -> p c t i", i=4)
                if eng == "G":
                    nc.gpsimd.tensor_scalar(out=dst, in0=src, scalar1=1.0, scalar2=-0.0, op0=MUL, op1=ADD)
                else:
                    copy(out=dst, in_=src)
            elif kind == "OQ":
                q, gp = ix
                key = "c%d%d" % (q // 2, gp)
                if key not in live:
                    live[key] = keep.tile([P, 512], U32, align_bytes=64, name="o" + key)
                c = 256 * (q % 2)
                nc.vector.quantize_mx(
                    out=live[key][:, c : c + 256].bitcast(E4M3),
                    scales=osc[q // 2][:, gp, c : c + 256],
                    in_=live[token[2:4]][:].rearrange("p o t -> p (o t)"),
                )
            elif kind == "SD":
                hh, gp = ix
                dst = out_1[gp].rearrange("p m t -> p (m t)")[:, 2048 * hh : 2048 * (hh + 1)]
                nc.sync.dma_start(out=dst.bitcast(I32), in_=live["c%d%d" % (hh, gp)][:].bitcast(I32))
            elif kind in ("SF", "SG"):
                hh, gp = ix[0] if kind == "SF" else 1, ix[1]
                c0, c1 = (0, 512) if kind == "SF" else (256 * (ix[0] - 2), 256 * (ix[0] - 1))
                dst = out_0[512 * gp : 512 * (gp + 1), 512 * hh + c0 : 512 * hh + c1].rearrange("(p t) o -> p t o", t=4)
                nc.sync.dma_start(out=dst, in_=of[hh][gp][:, :, c0:c1])
            elif kind == "SS":
                hh = ix[0]
                for q in range(4):
                    dst = out_2[:, 4 * q : 4 * q + 4, 512 * hh : 512 * (hh + 1)].bitcast(I32).rearrange("g q m -> q g m")
                    queue = nc.scalar if (q % 2 and hh == 1) else nc.sync
                    queue.dma_start(out=dst, in_=osc[hh][32 * q : 32 * q + 4, :, :].bitcast(I32))
            else:
                raise ValueError(token)

        for item in ORDER.split():
            token, eng = item.split(".")
            run(mark(token), eng)
